import numpy as np
import ml_dtypes


def mxq(x, axis, fmt="e4m3"):
    dtype, down = {"e4m3": (ml_dtypes.float8_e4m3fn, 7), "e5m2": (ml_dtypes.float8_e5m2, 14)}[fmt]
    v = np.moveaxis(np.asarray(x, np.float32).astype(ml_dtypes.bfloat16).astype(np.float64), axis, -1)
    blocks = v.reshape(v.shape[:-1] + (-1, 32))
    amax = np.abs(blocks).max(-1, keepdims=True)
    byte = np.maximum(np.where(amax > 0, np.frexp(amax)[1] - 1 + 127, 0) - down, 1)
    scale = np.exp2(byte - 127.0)
    codes = (blocks / scale).astype(np.float32).astype(dtype).astype(np.float64)
    return np.moveaxis((codes * scale).reshape(v.shape), -1, axis)


WIDE = False


def mx_kscale(k):
    if not WIDE:
        return np.ones(k)
    levels = np.array([10, -10, 5, -5, 0])
    if k % 512:
        return np.exp2(np.random.permutation(np.resize(levels, k // 32))).repeat(32)
    a = np.empty((k // 512, 16))
    for p in range(k // 512):
        a[p, :8] = np.random.permutation(np.resize(levels, 8))
        for g in range(8):
            far = levels[np.abs(levels - a[p, g]) >= 10]
            a[p, g + 8] = far[np.random.randint(len(far))]
    return np.exp2(a.ravel()).repeat(32)


BF16 = ml_dtypes.bfloat16


def bf(x):
    return np.asarray(x, np.float32).astype(BF16)


def f64(x):
    return np.asarray(x).astype(np.float64)


E2M1 = np.array([0.0, 0.5, 1.0, 1.5, 2.0, 3.0, 4.0, 6.0, -0.0, -0.5, -1.0, -1.5, -2.0, -3.0, -4.0, -6.0])


def pack_weight(w, fmt):
    k, n = w.shape
    w = f64(bf(w)).reshape(k // 32, 32, n)
    amax = np.abs(w).max(1)
    if fmt == "e4m3":
        byte = np.frexp(amax)[1] - 1 + 127 - 7
    else:
        mant, ex = np.frexp(amax / 6.0)
        byte = np.where(mant > 0.5, ex, ex - 1) + 127
    byte = np.clip(np.where(amax > 0, byte, 1), 1, 254)
    scaled = (w * np.exp2(127.0 - byte)[:, None, :]).reshape(k, n).astype(np.float32)
    by_word = np.ascontiguousarray(scaled.reshape(k // 512, 128, 4, n).transpose(0, 1, 3, 2))
    if fmt == "e4m3":
        words = by_word.astype(ml_dtypes.float8_e4m3fn).view(np.uint8)
    else:
        c = by_word.astype(ml_dtypes.float4_e2m1fn).view(np.uint8) & 0xF
        words = c[..., 0::2] | (c[..., 1::2] << 4)
    return np.ascontiguousarray(words), np.ascontiguousarray(byte.astype(np.uint8).reshape(k // 512, 16, n))


def unpack_weight(words, scales, fmt):
    g, p, n, _ = words.shape
    if fmt == "e4m3":
        vals = np.ascontiguousarray(words).view(ml_dtypes.float8_e4m3fn).astype(np.float64)
    else:
        nib = np.empty((g, p, n, 4), np.uint8)
        nib[..., 0::2] = words & 0xF
        nib[..., 1::2] = words >> 4
        vals = E2M1[nib]
    vals = vals * np.repeat(np.exp2(scales.astype(np.float64) - 127.0), 8, axis=1)[..., None]
    return vals.transpose(0, 1, 3, 2).reshape(g * 512, n)
def pack4(w):
    words, scales = pack_weight(w, "e2m1")
    return words.reshape(words.shape[0], 128, -1), scales


def unpack4(words, scales):
    return unpack_weight(words.reshape(words.shape[0], 128, -1, 2), scales, "e2m1")


T, C, B, N, Z = 1024, 512, 1024, 2048, 512


def setup_inputs():
    s = mx_kscale(C)
    u = mx_kscale(B)
    t = mx_kscale(N)
    loss_words, loss_scales = pack4(np.random.standard_normal((B, N)) / np.sqrt(B) / u[:, None] * t)
    pos_words, pos_scales = pack4(np.random.standard_normal((N, Z)) / np.sqrt(N) / t[:, None])
    return {"mu": bf(np.random.standard_normal((T, C)) * s),
            "shift": bf(np.random.standard_normal((N, C)) / np.sqrt(C) / s * t[:, None]),
            "flow": bf(np.random.standard_normal((T, B)) * u),
            "loss_words": loss_words,
            "loss_scales": loss_scales,
            "energy": bf(1 + 0.3 * np.random.standard_normal(T)),
            "delivery": bf((1 + 0.1 * np.random.standard_normal(N)) * t),
            "pos_words": pos_words,
            "pos_scales": pos_scales,
            "strike": bf(0.3 * np.random.standard_normal(Z))}


def reference(mu, shift, flow, loss_words, loss_scales, energy, delivery, pos_words, pos_scales, strike):
    congestion = mxq(f64(mu), 1, "e4m3") @ mxq(f64(shift), 1, "e4m3").T
    losses = mxq(f64(flow), 1, "e4m3") @ unpack4(loss_words, loss_scales)
    lmp = congestion + losses + f64(energy)[:, None] * f64(delivery)
    value = mxq(lmp, 1, "e4m3") @ unpack4(pos_words, pos_scales)
    return np.maximum(value - f64(strike), 0)

@@ -1,0 +1,288 @@
+from contextlib import ExitStack
+
+import concourse.mybir as mybir
+from concourse.masks import make_identity
+
+T, C, B, N, Z = 1024, 512, 1024, 2048, 512
+FLOPS = 2 * T * N * (C + B) + 2 * T * N * Z
+
+F32 = mybir.dt.float32
+BF16 = mybir.dt.bfloat16
+I32 = mybir.dt.int32
+U32 = mybir.dt.uint32
+U8 = mybir.dt.uint8
+FP8X4 = mybir.dt.float8_e4m3fn_x4
+FP4X4 = mybir.dt.float4_e2m1fn_x4
+ALU = mybir.AluOpType
+
+P = 128
+K_PASS = 512
+BANK = 512
+TILES = T // P
+CHUNKS = N // K_PASS
+PSUM_BANKS = 8
+QUANT_LAG = 2
+
+
+def tile_nodal_price_baskets_s3_kernel(
+    tc, mu, shift, flow, loss_words, loss_scales, energy, delivery, pos_words, pos_scales, strike, out
+):
+    nc = tc.nc
+    with ExitStack() as ctx:
+        keep = ctx.enter_context(tc.tile_pool(name="keep", bufs=1))
+        stage = ctx.enter_context(tc.tile_pool(name="stage", bufs=6))
+        psum = ctx.enter_context(tc.psum_pool(name="psum", bufs=1))
+        ctx.enter_context(tc.manual_schedule())
+
+        def kept(name, shape, dtype):
+            return keep.tile(shape, dtype, name=name, align_bytes=64)
+
+        ident = kept("ident", [P, P], F32)
+        make_identity(nc, ident[:])
+
+        loss_plane = kept("loss_plane", [P, B // K_PASS, N], U8)
+        pos_plane = kept("pos_plane", [P, CHUNKS, Z], U8)
+        nc.vector.memset(loss_plane[:].bitcast(U32), 0)
+        nc.vector.memset(pos_plane[:].bitcast(U32), 0)
+
+        def load_plane(queue, plane, rows):
+            for q in range(4):
+                queue.dma_start(
+                    out=plane[32 * q : 32 * q + 4].bitcast(I32),
+                    in_=rows[:, 4 * q : 4 * q + 4, :].rearrange("g r n -> r g n").bitcast(I32),
+                )
+
+        def load(name, src, dtype, queue=nc.sync):
+            dst = kept(name, list(src.shape), dtype)
+            if dtype is U8:
+                queue.dma_start(out=dst[:].bitcast(I32), in_=src.bitcast(I32))
+            else:
+                queue.dma_start(out=dst[:], in_=src)
+            return dst
+
+        mu_rows = mu.rearrange("(p i) c -> p i c", i=TILES)
+        flow_rows = flow.rearrange("(p i) b -> p i b", i=TILES)
+        out_rows = out.rearrange("(p i) z -> p i z", i=TILES)
+        shift_rows = shift.rearrange("(h p r) c -> h p r c", p=P, r=2)
+        loss_rows = loss_words.rearrange("g p b -> p g b")
+
+        delivery_raw = load("delivery_raw", delivery.rearrange("(p w) -> p w", p=P), BF16, nc.scalar)
+        energy_col = load("energy_col", energy.rearrange("(p i) -> p i", p=P), BF16, nc.scalar)
+        load_plane(nc.gpsimd, loss_plane, loss_scales)
+
+        mu_raw, flow_raw, shift_raw, loss_codes = {}, {}, {}, {}
+
+        def load_hours(pair):
+            mu_raw[pair] = load("mu_raw%d" % pair, mu_rows[:, 2 * pair : 2 * pair + 2, :], BF16)
+
+        def load_flow(i):
+            flow_raw[i] = load("flow_raw%d" % i, flow_rows[:, i, :], BF16)
+
+        def load_shift(j):
+            for h in (2 * j, 2 * j + 1):
+                shift_raw[h] = load("shift_raw%d" % h, shift_rows[h], BF16)
+
+        def load_loss(j):
+            loss_codes[j] = load("loss_codes%d" % j, loss_rows[:, :, 2 * K_PASS * j : 2 * K_PASS * (j + 1)], U8)
+
+        load_hours(0)
+        load_shift(0)
+        load_flow(0)
+        load_flow(1)
+        load_loss(0)
+        load_shift(1)
+        load_loss(1)
+        load_hours(1)
+        load_flow(2)
+        load_flow(3)
+        load_shift(2)
+        load_loss(2)
+        load_shift(3)
+        load_loss(3)
+        load_hours(2)
+        load_flow(4)
+        load_flow(5)
+        strike_raw = load("strike_raw", strike.rearrange("(p w) -> p w", p=P), BF16)
+        pos_codes = load("pos_codes", pos_words.rearrange("g p b -> p g b"), U8)
+        load_plane(nc.sync, pos_plane, pos_scales)
+        load_hours(3)
+        load_flow(6)
+        load_flow(7)
+
+        banks_used = []
+
+        def next_bank():
+            n = len(banks_used)
+            banks_used.append(n)
+            return psum.tile([P, BANK], F32, name="bank_%d" % n, tag="bank%d" % (n % PSUM_BANKS))
+
+        operands = {}
+        pending = []
+
+        def defer(key, work):
+            pending.append((key, len(banks_used), work))
+
+        def flush(keys=(), lag=None):
+            while pending and (
+                any(key in keys for key, born, work in pending)
+                or (lag is not None and len(banks_used) - pending[0][1] >= lag)
+            ):
+                pending.pop(0)[2]()
+
+        def turn(key, sources, order, codes, scales):
+            bank = next_bank()
+            width = P * len(sources)
+            for s, src in enumerate(sources):
+                nc.tensor.transpose(bank[:, P * s : P * (s + 1)], src, ident[:])
+            grouped = stage.tile([P, 2 * width], BF16, name="grouped_%s%d" % key, tag="grouped", align_bytes=64)
+            words = grouped[:].bitcast(F32)
+            if order == "columns":
+                nc.scalar.copy(
+                    out=words.rearrange("p (a c u) -> p a c u", c=P, u=2),
+                    in_=bank[:, :width].rearrange("p (a u c) -> p a c u", c=P, u=2),
+                )
+            else:
+                nc.scalar.copy(
+                    out=words.rearrange("p (c s) -> p c s", c=P),
+                    in_=bank[:, :width].rearrange("p (s c) -> p c s", c=P),
+                )
+            flush(lag=QUANT_LAG)
+            defer(key, lambda: nc.vector.quantize_mx(out=codes.bitcast(FP8X4), scales=scales, in_=grouped[:]))
+
+        def new_operand(key, width):
+            codes = kept("codes_%s%d" % key, [P, width], U32)
+            scales = kept("scales_%s%d" % key, [P, width], U8)
+            operands[key] = (codes, scales)
+            return codes, scales
+
+        def turn_mu(pair):
+            words = mu_raw[pair][:].bitcast(F32)
+            codes, scales = new_operand(("mu", pair), 2 * P)
+            turn(("mu", pair), [words[:, r, u::2] for r in range(2) for u in range(2)], "columns", codes[:], scales[:])
+
+        def turn_flow(i):
+            words = flow_raw[i][:].bitcast(F32).rearrange("p (g w) -> p g w", g=2)
+            codes, scales = new_operand(("flow", i), 2 * P)
+            turn(("flow", i), [words[:, g, u::2] for g in range(2) for u in range(2)], "columns", codes[:], scales[:])
+
+        def turn_shift(j):
+            codes, scales = new_operand(("shift", j), K_PASS)
+            for h in range(2):
+                words = shift_raw[2 * j + h][:].bitcast(F32)
+                cols = slice(2 * P * h, 2 * P * (h + 1))
+                turn(
+                    ("shift", j), [words[:, r, u::2] for r in range(2) for u in range(2)], "rows",
+                    codes[:, cols], scales[:, cols],
+                )
+
+        lmp = {}
+
+        def turn_lmp(i, chunks):
+            key = ("lmp", CHUNKS * i + chunks[0])
+            codes, scales = new_operand(key, P * len(chunks))
+            sources = []
+            for a, j in enumerate(chunks):
+                operands[("lmp", i, j)] = (key, codes[:, P * a : P * (a + 1)], scales[:, P * a : P * (a + 1)])
+                words = lmp[(i, j)][:].bitcast(F32)
+                sources.extend([words[:, P * u : P * (u + 1)] for u in range(2)])
+            turn(key, sources, "columns", codes[:], scales[:])
+
+        delivery_row = kept("delivery_row", [P, N], BF16)
+        strike_row = kept("strike_row", [P, Z], BF16)
+
+        def spread_delivery():
+            words = delivery_raw[:].bitcast(F32)
+            rows = delivery_row[:].bitcast(F32).rearrange("m (j u q v) -> m u j q v", j=CHUNKS, u=2, v=4)
+            for u in range(2):
+                bank = next_bank()
+                for v in range(4):
+                    w = 2 * v + u
+                    nc.tensor.transpose(bank[:, P * v : P * (v + 1)], words[:, w : w + 1].to_broadcast([P, P]), ident[:])
+                nc.vector.tensor_copy(out=rows[:, u], in_=bank[:].rearrange("m (v j q) -> m j q v", v=4, j=CHUNKS))
+
+        def spread_strike():
+            words = strike_raw[:].bitcast(F32)
+            bank = next_bank()
+            for w in range(2):
+                nc.tensor.transpose(bank[:, P * w : P * (w + 1)], words[:, w : w + 1].to_broadcast([P, P]), ident[:])
+            nc.scalar.copy(
+                out=strike_row[:].bitcast(F32).rearrange("m (q w) -> m q w", w=2),
+                in_=bank[:, : 2 * P].rearrange("m (w q) -> m q w", w=2),
+            )
+
+        def prices(i, j):
+            flush([("mu", i // 2), ("flow", i), ("shift", j)])
+            bank = next_bank()
+            cols = slice(P * (i % 2), P * (i % 2 + 1))
+            mu_codes, mu_scales = operands[("mu", i // 2)]
+            shift_codes, shift_scales = operands[("shift", j)]
+            flow_codes, flow_scales = operands[("flow", i)]
+            nc.tensor.matmul_mx(
+                out=bank[:], lhsT=mu_codes[:, cols].bitcast(FP8X4), lhsT_scale=mu_scales[:, cols],
+                rhs=shift_codes[:].bitcast(FP8X4), rhs_scale=shift_scales[:], start=True, stop=False,
+            )
+            for g in range(2):
+                cols = slice(P * g, P * (g + 1))
+                nc.tensor.matmul_mx(
+                    out=bank[:], lhsT=flow_codes[:, cols].bitcast(FP8X4), lhsT_scale=flow_scales[:, cols],
+                    rhs=loss_codes[j][:, g, :].bitcast(FP4X4),
+                    rhs_scale=loss_plane[:, g, K_PASS * j : K_PASS * (j + 1)], start=False, stop=(g == 1),
+                )
+            flush(lag=QUANT_LAG)
+            lmp[(i, j)] = stage.tile([P, K_PASS], BF16, name="lmp_%d_%d" % (i, j), tag="lmp", bufs=16, align_bytes=64)
+            sums = bank[:].rearrange("t (q u e) -> t u q e", u=2, e=2)
+            sorted_lmp = lmp[(i, j)][:].rearrange("t (u q e) -> t u q e", u=2, e=2)
+            sorted_delivery = delivery_row[:, K_PASS * j : K_PASS * (j + 1)].rearrange("t (u q e) -> t u q e", u=2, e=2)
+            for u in range(2):
+                nc.vector.scalar_tensor_tensor(
+                    out=sorted_lmp[:, u], in0=sorted_delivery[:, u], scalar=energy_col[:, i : i + 1], in1=sums[:, u],
+                    op0=ALU.mult, op1=ALU.add,
+                )
+
+        def payoffs(i, parts=1, lag=QUANT_LAG):
+            flush([operands[("lmp", i, j)][0] for j in range(CHUNKS)])
+            bank = next_bank()
+            for j in range(CHUNKS):
+                key, codes, scales = operands[("lmp", i, j)]
+                nc.tensor.matmul_mx(
+                    out=bank[:], lhsT=codes.bitcast(FP8X4), lhsT_scale=scales,
+                    rhs=pos_codes[:, j, :].bitcast(FP4X4), rhs_scale=pos_plane[:, j, :],
+                    start=(j == 0), stop=(j == CHUNKS - 1),
+                )
+            flush(lag=lag)
+            width = Z // parts
+            results = []
+            for s in range(parts):
+                cols = slice(width * s, width * (s + 1))
+                result = stage.tile([P, width], F32, name="result_%d_%d" % (i, s), tag="result", bufs=4)
+                nc.vector.tensor_tensor(out=result[:], in0=bank[:, cols], in1=strike_row[:, cols], op=ALU.subtract)
+                results.append((result, cols))
+            def finish():
+                for result, cols in results:
+                    nc.vector.tensor_scalar_max(out=result[:], in0=result[:], scalar1=0.0)
+                    nc.sync.dma_start(out=out_rows[:, i, cols], in_=result[:])
+            defer(("out", i), finish)
+
+        def run(turns, products):
+            for work in turns:
+                work[0](*work[1:])
+            for work in products:
+                work[0](*work[1:])
+
+        run(
+            [(spread_delivery,), (turn_mu, 0), (turn_shift, 0), (turn_flow, 0), (turn_flow, 1), (turn_shift, 1)],
+            [(prices, 0, 0), (prices, 1, 0)],
+        )
+        run([(turn_mu, 1), (turn_flow, 2), (turn_flow, 3)], [(prices, 0, 1), (prices, 1, 1)])
+        run([(turn_shift, 2), (turn_lmp, 0, (0, 1))], [(prices, 2, 0), (prices, 3, 0), (prices, 2, 1), (prices, 3, 1)])
+        run([(turn_shift, 3), (turn_lmp, 1, (0, 1)), (turn_lmp, 2, (0, 1))], [(prices, i, 2) for i in range(4)])
+        run([(turn_mu, 2), (turn_flow, 4), (turn_lmp, 3, (0, 1)), (spread_strike,)], [(prices, i, 3) for i in range(4)])
+        run([(turn_flow, 5), (turn_lmp, 0, (2, 3)), (turn_lmp, 1, (2, 3)), (turn_lmp, 2, (2, 3))],
+            [(prices, 4, j) for j in range(4)] + [(payoffs, 0), (payoffs, 1)])
+        run([(turn_mu, 3), (turn_flow, 6), (turn_lmp, 3, (2, 3)), (turn_lmp, 4, (0, 1)), (turn_lmp, 4, (2, 3))],
+            [(prices, 5, j) for j in range(4)] + [(payoffs, 2), (payoffs, 3)])
+        run([(turn_flow, 7), (turn_lmp, 5, (0, 1)), (turn_lmp, 5, (2, 3))],
+            [(prices, 6, j) for j in range(4)] + [(payoffs, 4)])
+        run([(turn_lmp, 6, (0, 1)), (turn_lmp, 6, (2, 3))], [(prices, 7, j) for j in range(4)] + [(payoffs, 5)])
+        run([(turn_lmp, 7, (0, 1)), (turn_lmp, 7, (2, 3))], [(payoffs, 6, 1, 1), (payoffs, 7, 2, 0)])
+        flush(lag=0)

@@ -14,6 +14,7 @@ U8 = mybir.dt.uint8
 FP8X4 = mybir.dt.float8_e4m3fn_x4
 FP4X4 = mybir.dt.float4_e2m1fn_x4
 ALU = mybir.AluOpType
+ACT = mybir.ActivationFunctionType
 
 P = 128
 K_PASS = 512
@@ -40,16 +41,16 @@ def tile_nodal_price_baskets_s3_kernel(
         ident = kept("ident", [P, P], F32)
         make_identity(nc, ident[:])
 
-        loss_plane = kept("loss_plane", [P, B // K_PASS, N], U8)
+        loss_planes = [kept("loss_plane%d" % h, [P, B // K_PASS, N // 2], U8) for h in range(2)]
         pos_plane = kept("pos_plane", [P, CHUNKS, Z], U8)
-        nc.vector.memset(loss_plane[:].bitcast(U32), 0)
-        nc.vector.memset(pos_plane[:].bitcast(U32), 0)
+        for plane in loss_planes + [pos_plane]:
+            nc.vector.memset(plane[:].bitcast(U32), 0)
 
-        def load_plane(queue, plane, rows):
+        def load_plane(plane, rows, cols):
             for q in range(4):
-                queue.dma_start(
+                nc.sync.dma_start(
                     out=plane[32 * q : 32 * q + 4].bitcast(I32),
-                    in_=rows[:, 4 * q : 4 * q + 4, :].rearrange("g r n -> r g n").bitcast(I32),
+                    in_=rows[:, 4 * q : 4 * q + 4, cols].rearrange("g r n -> r g n").bitcast(I32),
                 )
 
         def load(name, src, dtype, queue=nc.sync):
@@ -66,9 +67,8 @@ def tile_nodal_price_baskets_s3_kernel(
         shift_rows = shift.rearrange("(h p r) c -> h p r c", p=P, r=2)
         loss_rows = loss_words.rearrange("g p b -> p g b")
 
+        strike_raw = load("strike_raw", strike.rearrange("(p w) -> p w", p=P), BF16, nc.scalar)
         delivery_raw = load("delivery_raw", delivery.rearrange("(p w) -> p w", p=P), BF16, nc.scalar)
-        energy_col = load("energy_col", energy.rearrange("(p i) -> p i", p=P), BF16, nc.scalar)
-        load_plane(nc.gpsimd, loss_plane, loss_scales)
 
         mu_raw, flow_raw, shift_raw, loss_codes = {}, {}, {}, {}
 
@@ -89,22 +89,24 @@ def tile_nodal_price_baskets_s3_kernel(
         load_shift(0)
         load_flow(0)
         load_flow(1)
-        load_loss(0)
         load_shift(1)
-        load_loss(1)
+        load_loss(0)
+        energy_col = load("energy_col", energy.rearrange("(p i) -> p i", p=P), BF16)
+        load_plane(loss_planes[0], loss_scales, slice(0, N // 2))
         load_hours(1)
         load_flow(2)
+        load_loss(1)
         load_flow(3)
         load_shift(2)
         load_loss(2)
+        load_plane(loss_planes[1], loss_scales, slice(N // 2, N))
         load_shift(3)
         load_loss(3)
         load_hours(2)
         load_flow(4)
         load_flow(5)
-        strike_raw = load("strike_raw", strike.rearrange("(p w) -> p w", p=P), BF16)
         pos_codes = load("pos_codes", pos_words.rearrange("g p b -> p g b"), U8)
-        load_plane(nc.sync, pos_plane, pos_scales)
+        load_plane(pos_plane, pos_scales, slice(0, Z))
         load_hours(3)
         load_flow(6)
         load_flow(7)
@@ -129,7 +131,7 @@ def tile_nodal_price_baskets_s3_kernel(
             ):
                 pending.pop(0)[2]()
 
-        def turn(key, sources, order, codes, scales):
+        def turn(key, sources, order, codes, scales, copy_out=nc.scalar.copy):
             bank = next_bank()
             width = P * len(sources)
             for s, src in enumerate(sources):
@@ -137,12 +139,12 @@ def tile_nodal_price_baskets_s3_kernel(
             grouped = stage.tile([P, 2 * width], BF16, name="grouped_%s%d" % key, tag="grouped", align_bytes=64)
             words = grouped[:].bitcast(F32)
             if order == "columns":
-                nc.scalar.copy(
+                copy_out(
                     out=words.rearrange("p (a c u) -> p a c u", c=P, u=2),
                     in_=bank[:, :width].rearrange("p (a u c) -> p a c u", c=P, u=2),
                 )
             else:
-                nc.scalar.copy(
+                copy_out(
                     out=words.rearrange("p (c s) -> p c s", c=P),
                     in_=bank[:, :width].rearrange("p (s c) -> p c s", c=P),
                 )
@@ -155,29 +157,38 @@ def tile_nodal_price_baskets_s3_kernel(
             operands[key] = (codes, scales)
             return codes, scales
 
+        in_order = {}
+
+        def sort(engine_copy, key):
+            raw = {"mu": mu_raw, "flow": flow_raw, "shift": shift_raw}[key[0]][key[1]]
+            words = raw[:].bitcast(F32)
+            if key[0] != "flow":
+                words = words.rearrange("p r w -> p (r w)")
+            tile = stage.tile([P, BANK], F32, name="sorted_%s%d" % key, tag="sorted", bufs=8)
+            engine_copy(
+                out=tile[:].rearrange("p (a u c i) -> p a c u i", a=2, u=2, i=4),
+                in_=words.rearrange("p (a c i u) -> p a c u i", a=2, u=2, i=4),
+            )
+            in_order[key] = [tile[:, P * s : P * (s + 1)] for s in range(4)]
+
         def turn_mu(pair):
-            words = mu_raw[pair][:].bitcast(F32)
             codes, scales = new_operand(("mu", pair), 2 * P)
-            turn(("mu", pair), [words[:, r, u::2] for r in range(2) for u in range(2)], "columns", codes[:], scales[:])
+            turn(("mu", pair), in_order[("mu", pair)], "columns", codes[:], scales[:])
 
         def turn_flow(i):
-            words = flow_raw[i][:].bitcast(F32).rearrange("p (g w) -> p g w", g=2)
             codes, scales = new_operand(("flow", i), 2 * P)
-            turn(("flow", i), [words[:, g, u::2] for g in range(2) for u in range(2)], "columns", codes[:], scales[:])
+            turn(("flow", i), in_order[("flow", i)], "columns", codes[:], scales[:])
 
-        def turn_shift(j):
-            codes, scales = new_operand(("shift", j), K_PASS)
-            for h in range(2):
-                words = shift_raw[2 * j + h][:].bitcast(F32)
-                cols = slice(2 * P * h, 2 * P * (h + 1))
-                turn(
-                    ("shift", j), [words[:, r, u::2] for r in range(2) for u in range(2)], "rows",
-                    codes[:, cols], scales[:, cols],
-                )
+        def turn_shift(h):
+            if h % 2 == 0:
+                new_operand(("shift", h // 2), K_PASS)
+            codes, scales = operands[("shift", h // 2)]
+            cols = slice(2 * P * (h % 2), 2 * P * (h % 2 + 1))
+            turn(("shift", h // 2), in_order[("shift", h)], "rows", codes[:, cols], scales[:, cols])
 
-        lmp = {}
+        lmp, open_banks = {}, {}
 
-        def turn_lmp(i, chunks):
+        def turn_lmp(i, chunks, copy_out=nc.scalar.copy):
             key = ("lmp", CHUNKS * i + chunks[0])
             codes, scales = new_operand(key, P * len(chunks))
             sources = []
@@ -185,7 +196,7 @@ def tile_nodal_price_baskets_s3_kernel(
                 operands[("lmp", i, j)] = (key, codes[:, P * a : P * (a + 1)], scales[:, P * a : P * (a + 1)])
                 words = lmp[(i, j)][:].bitcast(F32)
                 sources.extend([words[:, P * u : P * (u + 1)] for u in range(2)])
-            turn(key, sources, "columns", codes[:], scales[:])
+            turn(key, sources, "columns", codes[:], scales[:], copy_out)
 
         delivery_row = kept("delivery_row", [P, N], BF16)
         strike_row = kept("strike_row", [P, Z], BF16)
@@ -198,35 +209,43 @@ def tile_nodal_price_baskets_s3_kernel(
                 for v in range(4):
                     w = 2 * v + u
                     nc.tensor.transpose(bank[:, P * v : P * (v + 1)], words[:, w : w + 1].to_broadcast([P, P]), ident[:])
-                nc.vector.tensor_copy(out=rows[:, u], in_=bank[:].rearrange("m (v j q) -> m j q v", v=4, j=CHUNKS))
+                nc.scalar.copy(out=rows[:, u], in_=bank[:].rearrange("m (v j q) -> m j q v", v=4, j=CHUNKS))
 
         def spread_strike():
             words = strike_raw[:].bitcast(F32)
             bank = next_bank()
             for w in range(2):
                 nc.tensor.transpose(bank[:, P * w : P * (w + 1)], words[:, w : w + 1].to_broadcast([P, P]), ident[:])
-            nc.scalar.copy(
-                out=strike_row[:].bitcast(F32).rearrange("m (q w) -> m q w", w=2),
-                in_=bank[:, : 2 * P].rearrange("m (w q) -> m q w", w=2),
+            nc.scalar.activation(
+                out=strike_row[:].rearrange("m (q w e) -> m q w e", w=2, e=2),
+                in_=bank[:, : 2 * P].bitcast(BF16).rearrange("m (w q e) -> m q w e", w=2, e=2),
+                func=ACT.Copy,
             )
 
-        def prices(i, j):
-            flush([("mu", i // 2), ("flow", i), ("shift", j)])
+        def congestion(i, j):
+            flush([("mu", i // 2), ("shift", j)])
             bank = next_bank()
             cols = slice(P * (i % 2), P * (i % 2 + 1))
             mu_codes, mu_scales = operands[("mu", i // 2)]
             shift_codes, shift_scales = operands[("shift", j)]
-            flow_codes, flow_scales = operands[("flow", i)]
             nc.tensor.matmul_mx(
                 out=bank[:], lhsT=mu_codes[:, cols].bitcast(FP8X4), lhsT_scale=mu_scales[:, cols],
                 rhs=shift_codes[:].bitcast(FP8X4), rhs_scale=shift_scales[:], start=True, stop=False,
             )
+            open_banks[(i, j)] = bank
+
+        def prices(i, j):
+            if (i, j) not in open_banks:
+                congestion(i, j)
+            flush([("flow", i)])
+            bank = open_banks[(i, j)]
+            flow_codes, flow_scales = operands[("flow", i)]
             for g in range(2):
                 cols = slice(P * g, P * (g + 1))
                 nc.tensor.matmul_mx(
                     out=bank[:], lhsT=flow_codes[:, cols].bitcast(FP8X4), lhsT_scale=flow_scales[:, cols],
                     rhs=loss_codes[j][:, g, :].bitcast(FP4X4),
-                    rhs_scale=loss_plane[:, g, K_PASS * j : K_PASS * (j + 1)], start=False, stop=(g == 1),
+                    rhs_scale=loss_planes[j // 2][:, g, K_PASS * (j % 2) : K_PASS * (j % 2 + 1)], start=False, stop=(g == 1),
                 )
             flush(lag=QUANT_LAG)
             lmp[(i, j)] = stage.tile([P, K_PASS], BF16, name="lmp_%d_%d" % (i, j), tag="lmp", bufs=16, align_bytes=64)
@@ -239,50 +258,72 @@ def tile_nodal_price_baskets_s3_kernel(
                     op0=ALU.mult, op1=ALU.add,
                 )
 
-        def payoffs(i, parts=1, lag=QUANT_LAG):
-            flush([operands[("lmp", i, j)][0] for j in range(CHUNKS)])
-            bank = next_bank()
-            for j in range(CHUNKS):
-                key, codes, scales = operands[("lmp", i, j)]
-                nc.tensor.matmul_mx(
-                    out=bank[:], lhsT=codes.bitcast(FP8X4), lhsT_scale=scales,
-                    rhs=pos_codes[:, j, :].bitcast(FP4X4), rhs_scale=pos_plane[:, j, :],
-                    start=(j == 0), stop=(j == CHUNKS - 1),
-                )
-            flush(lag=lag)
-            width = Z // parts
-            results = []
-            for s in range(parts):
-                cols = slice(width * s, width * (s + 1))
-                result = stage.tile([P, width], F32, name="result_%d_%d" % (i, s), tag="result", bufs=4)
-                nc.vector.tensor_tensor(out=result[:], in0=bank[:, cols], in1=strike_row[:, cols], op=ALU.subtract)
-                results.append((result, cols))
-            def finish():
-                for result, cols in results:
-                    nc.vector.tensor_scalar_max(out=result[:], in0=result[:], scalar1=0.0)
-                    nc.sync.dma_start(out=out_rows[:, i, cols], in_=result[:])
-            defer(("out", i), finish)
+        unclipped = []
 
-        def run(turns, products):
+        def clip_and_store():
+            while unclipped:
+                result, rows = unclipped.pop(0)
+                nc.scalar.activation(out=result[:], in_=result[:], func=ACT.Relu)
+                nc.sync.dma_start(out=rows, in_=result[:])
+
+        def payoffs(i, groups=1, parts=1, lag=QUANT_LAG):
+            width = Z // groups
+            banks = [next_bank() for s in range(groups)]
+            for half in range(2):
+                for s in range(groups):
+                    for j in (2 * half, 2 * half + 1):
+                        key, codes, scales = operands[("lmp", i, j)]
+                        flush([key])
+                        nc.tensor.matmul_mx(
+                            out=banks[s][:, :width], lhsT=codes.bitcast(FP8X4), lhsT_scale=scales,
+                            rhs=pos_codes[:, j, 2 * width * s : 2 * width * (s + 1)].bitcast(FP4X4),
+                            rhs_scale=pos_plane[:, j, width * s : width * (s + 1)],
+                            start=(j == 0), stop=(j == CHUNKS - 1),
+                        )
+            flush(lag=lag)
+            piece = Z // parts
+            for s in range(parts):
+                cols = slice(piece * s, piece * (s + 1))
+                first = piece * s % width
+                result = stage.tile([P, piece], F32, name="result_%d_%d" % (i, s), tag="result", bufs=8)
+                nc.vector.tensor_tensor(
+                    out=result[:], in0=banks[piece * s // width][:, first : first + piece], in1=strike_row[:, cols],
+                    op=ALU.subtract,
+                )
+                clip_and_store()
+                unclipped.append((result, out_rows[:, i, cols]))
+
+        def run(turns, products, sorts=()):
             for work in turns:
                 work[0](*work[1:])
+            clip_and_store()
+            for ahead in sorts:
+                sort(*ahead)
             for work in products:
                 work[0](*work[1:])
 
-        run(
-            [(spread_delivery,), (turn_mu, 0), (turn_shift, 0), (turn_flow, 0), (turn_flow, 1), (turn_shift, 1)],
-            [(prices, 0, 0), (prices, 1, 0)],
-        )
-        run([(turn_mu, 1), (turn_flow, 2), (turn_flow, 3)], [(prices, 0, 1), (prices, 1, 1)])
-        run([(turn_shift, 2), (turn_lmp, 0, (0, 1))], [(prices, 2, 0), (prices, 3, 0), (prices, 2, 1), (prices, 3, 1)])
-        run([(turn_shift, 3), (turn_lmp, 1, (0, 1)), (turn_lmp, 2, (0, 1))], [(prices, i, 2) for i in range(4)])
-        run([(turn_mu, 2), (turn_flow, 4), (turn_lmp, 3, (0, 1)), (spread_strike,)], [(prices, i, 3) for i in range(4)])
-        run([(turn_flow, 5), (turn_lmp, 0, (2, 3)), (turn_lmp, 1, (2, 3)), (turn_lmp, 2, (2, 3))],
-            [(prices, 4, j) for j in range(4)] + [(payoffs, 0), (payoffs, 1)])
-        run([(turn_mu, 3), (turn_flow, 6), (turn_lmp, 3, (2, 3)), (turn_lmp, 4, (0, 1)), (turn_lmp, 4, (2, 3))],
-            [(prices, 5, j) for j in range(4)] + [(payoffs, 2), (payoffs, 3)])
-        run([(turn_flow, 7), (turn_lmp, 5, (0, 1)), (turn_lmp, 5, (2, 3))],
-            [(prices, 6, j) for j in range(4)] + [(payoffs, 4)])
-        run([(turn_lmp, 6, (0, 1)), (turn_lmp, 6, (2, 3))], [(prices, 7, j) for j in range(4)] + [(payoffs, 5)])
-        run([(turn_lmp, 7, (0, 1)), (turn_lmp, 7, (2, 3))], [(payoffs, 6, 1, 1), (payoffs, 7, 2, 0)])
-        flush(lag=0)
+        V, S = nc.vector.tensor_copy, nc.scalar.copy
+        spread_strike()
+        spread_delivery()
+        first = [(("mu", 0), turn_mu), (("shift", 0), turn_shift), (("shift", 1), turn_shift), (("flow", 0), turn_flow),
+                 (("flow", 1), turn_flow), (("shift", 2), turn_shift), (("shift", 3), turn_shift)]
+        sort(V, first[0][0])
+        for n, (key, work) in enumerate(first[:-1]):
+            sort(V, first[n + 1][0])
+            work(key[1])
+        run([], [(congestion, 0, 0), (congestion, 1, 0)])
+        run([(turn_shift, 3)], [(prices, 0, 0), (flush, [("shift", 1)]), (prices, 1, 0)], [(V, ("mu", 1)), (V, ("flow", 2)), (S, ("flow", 3))])
+        run([(turn_mu, 1), (turn_flow, 2)], [(prices, 0, 1), (prices, 1, 1)], [(S, ("shift", 4)), (S, ("shift", 5))])
+        run([(turn_flow, 3), (turn_shift, 4), (turn_lmp, 0, (0, 1)), (turn_shift, 5), (turn_lmp, 1, (0, 1))],
+            [(prices, 2, 0), (prices, 2, 1), (prices, 3, 0), (prices, 3, 1)],
+            [(S, ("shift", 6)), (S, ("shift", 7)), (S, ("mu", 2)), (S, ("flow", 4))])
+        run([(turn_shift, 6), (turn_shift, 7), (turn_mu, 2), (turn_flow, 4), (turn_lmp, 2, (0, 1)), (turn_lmp, 3, (0, 1))],
+            [(prices, i, j) for j in (2, 3) for i in range(4)],
+            [(S, ("flow", 5)), (S, ("mu", 3)), (S, ("flow", 6)), (S, ("flow", 7))])
+        run([(turn_flow, 5), (turn_mu, 3), (turn_flow, 6), (turn_lmp, 0, (2, 3)), (turn_lmp, 1, (2, 3)), (turn_lmp, 2, (2, 3))],
+            [(prices, i, j) for i in (4, 5) for j in range(4)] + [(payoffs, 0), (payoffs, 1), (payoffs, 2)])
+        run([(turn_flow, 7), (turn_lmp, 3, (2, 3))] + [(turn_lmp, i, half) for i in (4, 5) for half in ((0, 1), (2, 3))],
+            [(prices, i, j) for i in (6, 7) for j in range(4)] + [(payoffs, 3), (payoffs, 4)])
+        run([(turn_lmp, 6, (0, 1), V), (turn_lmp, 6, (2, 3)), (turn_lmp, 7, (0, 1)), (turn_lmp, 7, (2, 3))],
+            [(payoffs, 5, 1, 1, 1), (payoffs, 6, 1, 2, 1), (payoffs, 7, 4, 4, 0)])
+        clip_and_store()

@@ -19,10 +19,12 @@ ACT = mybir.ActivationFunctionType
 P = 128
 K_PASS = 512
 BANK = 512
+SLAB = 2 * BANK
 TILES = T // P
 CHUNKS = N // K_PASS
 PSUM_BANKS = 8
 QUANT_LAG = 2
+ALIGN = 64
 
 
 def tile_nodal_price_baskets_s3_kernel(
@@ -36,7 +38,7 @@ def tile_nodal_price_baskets_s3_kernel(
         ctx.enter_context(tc.manual_schedule())
 
         def kept(name, shape, dtype):
-            return keep.tile(shape, dtype, name=name, align_bytes=64)
+            return keep.tile(shape, dtype, name=name, align_bytes=ALIGN)
 
         ident = kept("ident", [P, P], F32)
         make_identity(nc, ident[:])
@@ -46,11 +48,11 @@ def tile_nodal_price_baskets_s3_kernel(
         for plane in loss_planes + [pos_plane]:
             nc.vector.memset(plane[:].bitcast(U32), 0)
 
-        def load_plane(plane, rows, cols):
-            for q in range(4):
+        def load_plane(plane, scale_rows, cols):
+            for r in range(4):
                 nc.sync.dma_start(
-                    out=plane[32 * q : 32 * q + 4].bitcast(I32),
-                    in_=rows[:, 4 * q : 4 * q + 4, cols].rearrange("g r n -> r g n").bitcast(I32),
+                    out=plane[r:P:32].bitcast(I32),
+                    in_=scale_rows[:, r:16:4, cols].rearrange("g q n -> q g n").bitcast(I32),
                 )
 
         def load(name, src, dtype, queue=nc.sync):
@@ -61,55 +63,59 @@ def tile_nodal_price_baskets_s3_kernel(
                 queue.dma_start(out=dst[:], in_=src)
             return dst
 
-        mu_rows = mu.rearrange("(p i) c -> p i c", i=TILES)
-        flow_rows = flow.rearrange("(p i) b -> p i b", i=TILES)
+        rows = {
+            "mu": mu.rearrange("(p i) c -> p (i c)", i=TILES),
+            "flow": flow.rearrange("(p i) b -> p (i b)", i=TILES),
+        }
+        shift_rows = shift.rearrange("(h p r) c -> h p (r c)", p=P, r=2)
         out_rows = out.rearrange("(p i) z -> p i z", i=TILES)
-        shift_rows = shift.rearrange("(h p r) c -> h p r c", p=P, r=2)
         loss_rows = loss_words.rearrange("g p b -> p g b")
 
-        strike_raw = load("strike_raw", strike.rearrange("(p w) -> p w", p=P), BF16, nc.scalar)
         delivery_raw = load("delivery_raw", delivery.rearrange("(p w) -> p w", p=P), BF16, nc.scalar)
 
-        mu_raw, flow_raw, shift_raw, loss_codes = {}, {}, {}, {}
+        slabs, loss_codes = {}, {}
 
-        def load_hours(pair):
-            mu_raw[pair] = load("mu_raw%d" % pair, mu_rows[:, 2 * pair : 2 * pair + 2, :], BF16)
+        def load_slabs(name, first, count):
+            if name == "shift":
+                src = shift_rows[first]
+            else:
+                src = rows[name][:, SLAB * first : SLAB * (first + count)]
+            words = load("%s_raw%d" % (name, first), src, BF16)[:].bitcast(F32)
+            for n in range(count):
+                slabs[(name, first + n)] = words[:, BANK * n : BANK * (n + 1)]
 
-        def load_flow(i):
-            flow_raw[i] = load("flow_raw%d" % i, flow_rows[:, i, :], BF16)
+        def load_loss(first, count):
+            width = 2 * K_PASS
+            codes = load("loss_codes%d" % first, loss_rows[:, :, width * first : width * (first + count)], U8)
+            for n in range(count):
+                loss_codes[first + n] = codes[:, :, width * n : width * (n + 1)]
 
-        def load_shift(j):
-            for h in (2 * j, 2 * j + 1):
-                shift_raw[h] = load("shift_raw%d" % h, shift_rows[h], BF16)
-
-        def load_loss(j):
-            loss_codes[j] = load("loss_codes%d" % j, loss_rows[:, :, 2 * K_PASS * j : 2 * K_PASS * (j + 1)], U8)
-
-        load_hours(0)
-        load_shift(0)
-        load_flow(0)
-        load_flow(1)
-        load_shift(1)
-        load_loss(0)
-        energy_col = load("energy_col", energy.rearrange("(p i) -> p i", p=P), BF16)
+        load_slabs("mu", 0, 1)
+        load_slabs("shift", 0, 1)
+        load_slabs("shift", 1, 1)
+        load_slabs("flow", 0, 1)
+        load_slabs("flow", 1, 1)
+        load_slabs("shift", 2, 1)
+        load_slabs("shift", 3, 1)
         load_plane(loss_planes[0], loss_scales, slice(0, N // 2))
-        load_hours(1)
-        load_flow(2)
-        load_loss(1)
-        load_flow(3)
-        load_shift(2)
-        load_loss(2)
+        load_loss(0, 1)
+        energy_col = load("energy_col", energy.rearrange("(p i) -> p i", p=P), BF16)
+        load_slabs("mu", 1, 1)
+        load_slabs("flow", 2, 1)
+        load_loss(1, 1)
+        load_slabs("flow", 3, 1)
+        load_slabs("shift", 4, 1)
+        load_slabs("shift", 5, 1)
+        load_loss(2, 2)
         load_plane(loss_planes[1], loss_scales, slice(N // 2, N))
-        load_shift(3)
-        load_loss(3)
-        load_hours(2)
-        load_flow(4)
-        load_flow(5)
+        load_slabs("shift", 6, 1)
+        load_slabs("shift", 7, 1)
+        load_slabs("mu", 2, 2)
+        load_slabs("flow", 4, 2)
+        strike_raw = load("strike_raw", strike.rearrange("(p w) -> p w", p=P), BF16)
         pos_codes = load("pos_codes", pos_words.rearrange("g p b -> p g b"), U8)
         load_plane(pos_plane, pos_scales, slice(0, Z))
-        load_hours(3)
-        load_flow(6)
-        load_flow(7)
+        load_slabs("flow", 6, 2)
 
         banks_used = []
 
@@ -131,25 +137,24 @@ def tile_nodal_price_baskets_s3_kernel(
             ):
                 pending.pop(0)[2]()
 
-        def turn(key, sources, order, codes, scales, copy_out=nc.scalar.copy):
+        def transposed(sources):
             bank = next_bank()
-            width = P * len(sources)
             for s, src in enumerate(sources):
                 nc.tensor.transpose(bank[:, P * s : P * (s + 1)], src, ident[:])
-            grouped = stage.tile([P, 2 * width], BF16, name="grouped_%s%d" % key, tag="grouped", align_bytes=64)
-            words = grouped[:].bitcast(F32)
-            if order == "columns":
-                copy_out(
-                    out=words.rearrange("p (a c u) -> p a c u", c=P, u=2),
-                    in_=bank[:, :width].rearrange("p (a u c) -> p a c u", c=P, u=2),
-                )
-            else:
-                copy_out(
-                    out=words.rearrange("p (c s) -> p c s", c=P),
-                    in_=bank[:, :width].rearrange("p (s c) -> p c s", c=P),
-                )
-            flush(lag=QUANT_LAG)
+            return bank
+
+        def quantise_later(key, codes, scales, grouped):
             defer(key, lambda: nc.vector.quantize_mx(out=codes.bitcast(FP8X4), scales=scales, in_=grouped[:]))
+
+        def turn(key, sources, codes, scales, copy_out=nc.scalar.copy):
+            bank = transposed(sources)
+            grouped = stage.tile([P, SLAB], BF16, name="grouped_%s%d" % key, tag="grouped", align_bytes=ALIGN)
+            copy_out(
+                out=grouped[:].bitcast(F32).rearrange("p (a c u) -> p a c u", c=P, u=2),
+                in_=bank[:].rearrange("p (a u c) -> p a c u", c=P, u=2),
+            )
+            flush(lag=QUANT_LAG)
+            quantise_later(key, codes, scales, grouped)
 
         def new_operand(key, width):
             codes = kept("codes_%s%d" % key, [P, width], U32)
@@ -160,10 +165,7 @@ def tile_nodal_price_baskets_s3_kernel(
         in_order = {}
 
         def sort(engine_copy, key):
-            raw = {"mu": mu_raw, "flow": flow_raw, "shift": shift_raw}[key[0]][key[1]]
-            words = raw[:].bitcast(F32)
-            if key[0] != "flow":
-                words = words.rearrange("p r w -> p (r w)")
+            words = slabs[key]
             tile = stage.tile([P, BANK], F32, name="sorted_%s%d" % key, tag="sorted", bufs=8)
             engine_copy(
                 out=tile[:].rearrange("p (a u c i) -> p a c u i", a=2, u=2, i=4),
@@ -173,18 +175,26 @@ def tile_nodal_price_baskets_s3_kernel(
 
         def turn_mu(pair):
             codes, scales = new_operand(("mu", pair), 2 * P)
-            turn(("mu", pair), in_order[("mu", pair)], "columns", codes[:], scales[:])
+            turn(("mu", pair), in_order[("mu", pair)], codes[:], scales[:])
 
         def turn_flow(i):
             codes, scales = new_operand(("flow", i), 2 * P)
-            turn(("flow", i), in_order[("flow", i)], "columns", codes[:], scales[:])
+            turn(("flow", i), in_order[("flow", i)], codes[:], scales[:])
 
         def turn_shift(h):
+            j = h // 2
             if h % 2 == 0:
-                new_operand(("shift", h // 2), K_PASS)
-            codes, scales = operands[("shift", h // 2)]
+                new_operand(("shift", j), K_PASS)
+            codes, scales = operands[("shift", j)]
             cols = slice(2 * P * (h % 2), 2 * P * (h % 2 + 1))
-            turn(("shift", h // 2), in_order[("shift", h)], "rows", codes[:, cols], scales[:, cols])
+            bank = transposed(in_order[("shift", h)])
+            grouped = stage.tile([P, SLAB], BF16, name="grouped_shift%d" % h, tag="grouped", align_bytes=ALIGN)
+            nc.scalar.copy(
+                out=grouped[:].bitcast(F32).rearrange("p (c v) -> p c v", v=4),
+                in_=bank[:].rearrange("p (v c) -> p c v", c=P),
+            )
+            flush(lag=QUANT_LAG)
+            quantise_later(("shift", j), codes[:, cols], scales[:, cols], grouped)
 
         lmp, open_banks = {}, {}
 
@@ -196,7 +206,7 @@ def tile_nodal_price_baskets_s3_kernel(
                 operands[("lmp", i, j)] = (key, codes[:, P * a : P * (a + 1)], scales[:, P * a : P * (a + 1)])
                 words = lmp[(i, j)][:].bitcast(F32)
                 sources.extend([words[:, P * u : P * (u + 1)] for u in range(2)])
-            turn(key, sources, "columns", codes[:], scales[:], copy_out)
+            turn(key, sources, codes[:], scales[:], copy_out)
 
         delivery_row = kept("delivery_row", [P, N], BF16)
         strike_row = kept("strike_row", [P, Z], BF16)
@@ -248,7 +258,7 @@ def tile_nodal_price_baskets_s3_kernel(
                     rhs_scale=loss_planes[j // 2][:, g, K_PASS * (j % 2) : K_PASS * (j % 2 + 1)], start=False, stop=(g == 1),
                 )
             flush(lag=QUANT_LAG)
-            lmp[(i, j)] = stage.tile([P, K_PASS], BF16, name="lmp_%d_%d" % (i, j), tag="lmp", bufs=16, align_bytes=64)
+            lmp[(i, j)] = stage.tile([P, K_PASS], BF16, name="lmp_%d_%d" % (i, j), tag="lmp", bufs=16, align_bytes=ALIGN)
             sums = bank[:].rearrange("t (q u e) -> t u q e", u=2, e=2)
             sorted_lmp = lmp[(i, j)][:].rearrange("t (u q e) -> t u q e", u=2, e=2)
             sorted_delivery = delivery_row[:, K_PASS * j : K_PASS * (j + 1)].rearrange("t (u q e) -> t u q e", u=2, e=2)
@@ -303,7 +313,6 @@ def tile_nodal_price_baskets_s3_kernel(
                 work[0](*work[1:])
 
         V, S = nc.vector.tensor_copy, nc.scalar.copy
-        spread_strike()
         spread_delivery()
         first = [(("mu", 0), turn_mu), (("shift", 0), turn_shift), (("shift", 1), turn_shift), (("flow", 0), turn_flow),
                  (("flow", 1), turn_flow), (("shift", 2), turn_shift), (("shift", 3), turn_shift)]
@@ -320,7 +329,7 @@ def tile_nodal_price_baskets_s3_kernel(
         run([(turn_shift, 6), (turn_shift, 7), (turn_mu, 2), (turn_flow, 4), (turn_lmp, 2, (0, 1)), (turn_lmp, 3, (0, 1))],
             [(prices, i, j) for j in (2, 3) for i in range(4)],
             [(S, ("flow", 5)), (S, ("mu", 3)), (S, ("flow", 6)), (S, ("flow", 7))])
-        run([(turn_flow, 5), (turn_mu, 3), (turn_flow, 6), (turn_lmp, 0, (2, 3)), (turn_lmp, 1, (2, 3)), (turn_lmp, 2, (2, 3))],
+        run([(turn_flow, 5), (turn_mu, 3), (turn_flow, 6), (turn_lmp, 0, (2, 3)), (turn_lmp, 1, (2, 3)), (turn_lmp, 2, (2, 3)), (spread_strike,)],
             [(prices, i, j) for i in (4, 5) for j in range(4)] + [(payoffs, 0), (payoffs, 1), (payoffs, 2)])
         run([(turn_flow, 7), (turn_lmp, 3, (2, 3))] + [(turn_lmp, i, half) for i in (4, 5) for half in ((0, 1), (2, 3))],
             [(prices, i, j) for i in (6, 7) for j in range(4)] + [(payoffs, 3), (payoffs, 4)])

from contextlib import ExitStack

import concourse.mybir as mybir
from concourse.masks import make_identity

T, C, B, N, Z = 1024, 512, 1024, 2048, 512
FLOPS = 2 * T * N * (C + B) + 2 * T * N * Z

F32 = mybir.dt.float32
BF16 = mybir.dt.bfloat16
I32 = mybir.dt.int32
U32 = mybir.dt.uint32
U8 = mybir.dt.uint8
FP8X4 = mybir.dt.float8_e4m3fn_x4
FP4X4 = mybir.dt.float4_e2m1fn_x4
ALU = mybir.AluOpType
ACT = mybir.ActivationFunctionType

P = 128
K_PASS = 512
BANK = 512
SLAB = 2 * BANK
TILES = T // P
CHUNKS = N // K_PASS
PSUM_BANKS = 8
QUANT_LAG = 2
ALIGN = 64


def tile_nodal_price_baskets_s3_kernel(
    tc, mu, shift, flow, loss_words, loss_scales, energy, delivery, pos_words, pos_scales, strike, out
):
    nc = tc.nc
    with ExitStack() as ctx:
        keep = ctx.enter_context(tc.tile_pool(name="keep", bufs=1))
        stage = ctx.enter_context(tc.tile_pool(name="stage", bufs=6))
        psum = ctx.enter_context(tc.psum_pool(name="psum", bufs=1))
        ctx.enter_context(tc.manual_schedule())

        def kept(name, shape, dtype):
            return keep.tile(shape, dtype, name=name, align_bytes=ALIGN)

        ident = kept("ident", [P, P], F32)
        make_identity(nc, ident[:])

        loss_planes = [kept("loss_plane%d" % h, [P, B // K_PASS, N // 2], U8) for h in range(2)]
        pos_plane = kept("pos_plane", [P, CHUNKS, Z], U8)
        for plane in loss_planes + [pos_plane]:
            nc.vector.memset(plane[:].bitcast(U32), 0)

        def load_plane(plane, scale_rows, cols):
            for r in range(4):
                nc.sync.dma_start(
                    out=plane[r:P:32].bitcast(I32),
                    in_=scale_rows[:, r:16:4, cols].rearrange("g q n -> q g n").bitcast(I32),
                )

        def load(name, src, dtype, queue=nc.sync):
            dst = kept(name, list(src.shape), dtype)
            if dtype is U8:
                queue.dma_start(out=dst[:].bitcast(I32), in_=src.bitcast(I32))
            else:
                queue.dma_start(out=dst[:], in_=src)
            return dst

        rows = {
            "mu": mu.rearrange("(p i) c -> p (i c)", i=TILES),
            "flow": flow.rearrange("(p i) b -> p (i b)", i=TILES),
        }
        shift_rows = shift.rearrange("(h p r) c -> h p (r c)", p=P, r=2)
        out_rows = out.rearrange("(p i) z -> p i z", i=TILES)
        loss_rows = loss_words.rearrange("g p b -> p g b")

        delivery_raw = load("delivery_raw", delivery.rearrange("(p w) -> p w", p=P), BF16, nc.scalar)

        slabs, loss_codes = {}, {}

        def load_slabs(name, first, count):
            if name == "shift":
                src = shift_rows[first]
            else:
                src = rows[name][:, SLAB * first : SLAB * (first + count)]
            words = load("%s_raw%d" % (name, first), src, BF16)[:].bitcast(F32)
            for n in range(count):
                slabs[(name, first + n)] = words[:, BANK * n : BANK * (n + 1)]

        def load_loss(first, count):
            width = 2 * K_PASS
            codes = load("loss_codes%d" % first, loss_rows[:, :, width * first : width * (first + count)], U8)
            for n in range(count):
                loss_codes[first + n] = codes[:, :, width * n : width * (n + 1)]

        load_slabs("mu", 0, 1)
        load_slabs("shift", 0, 1)
        load_slabs("shift", 1, 1)
        load_slabs("flow", 0, 1)
        load_slabs("flow", 1, 1)
        load_slabs("shift", 2, 1)
        load_slabs("shift", 3, 1)
        load_plane(loss_planes[0], loss_scales, slice(0, N // 2))
        load_loss(0, 1)
        energy_col = load("energy_col", energy.rearrange("(p i) -> p i", p=P), BF16)
        load_slabs("mu", 1, 1)
        load_slabs("flow", 2, 1)
        load_loss(1, 1)
        load_slabs("flow", 3, 1)
        load_slabs("shift", 4, 1)
        load_slabs("shift", 5, 1)
        load_loss(2, 2)
        load_plane(loss_planes[1], loss_scales, slice(N // 2, N))
        load_slabs("shift", 6, 1)
        load_slabs("shift", 7, 1)
        load_slabs("mu", 2, 2)
        load_slabs("flow", 4, 2)
        strike_raw = load("strike_raw", strike.rearrange("(p w) -> p w", p=P), BF16)
        pos_codes = load("pos_codes", pos_words.rearrange("g p b -> p g b"), U8)
        load_plane(pos_plane, pos_scales, slice(0, Z))
        load_slabs("flow", 6, 2)

        banks_used = []

        def next_bank():
            n = len(banks_used)
            banks_used.append(n)
            return psum.tile([P, BANK], F32, name="bank_%d" % n, tag="bank%d" % (n % PSUM_BANKS))

        operands = {}
        pending = []

        def defer(key, work):
            pending.append((key, len(banks_used), work))

        def flush(keys=(), lag=None):
            while pending and (
                any(key in keys for key, born, work in pending)
                or (lag is not None and len(banks_used) - pending[0][1] >= lag)
            ):
                pending.pop(0)[2]()

        def transposed(sources):
            bank = next_bank()
            for s, src in enumerate(sources):
                nc.tensor.transpose(bank[:, P * s : P * (s + 1)], src, ident[:])
            return bank

        def quantise_later(key, codes, scales, grouped):
            defer(key, lambda: nc.vector.quantize_mx(out=codes.bitcast(FP8X4), scales=scales, in_=grouped[:]))

        def turn(key, sources, codes, scales, copy_out=nc.scalar.copy):
            bank = transposed(sources)
            grouped = stage.tile([P, SLAB], BF16, name="grouped_%s%d" % key, tag="grouped", align_bytes=ALIGN)
            copy_out(
                out=grouped[:].bitcast(F32).rearrange("p (a c u) -> p a c u", c=P, u=2),
                in_=bank[:].rearrange("p (a u c) -> p a c u", c=P, u=2),
            )
            flush(lag=QUANT_LAG)
            quantise_later(key, codes, scales, grouped)

        def new_operand(key, width):
            codes = kept("codes_%s%d" % key, [P, width], U32)
            scales = kept("scales_%s%d" % key, [P, width], U8)
            operands[key] = (codes, scales)
            return codes, scales

        in_order = {}

        def sort(engine_copy, key):
            words = slabs[key]
            tile = stage.tile([P, BANK], F32, name="sorted_%s%d" % key, tag="sorted", bufs=8)
            engine_copy(
                out=tile[:].rearrange("p (a u c i) -> p a c u i", a=2, u=2, i=4),
                in_=words.rearrange("p (a c i u) -> p a c u i", a=2, u=2, i=4),
            )
            in_order[key] = [tile[:, P * s : P * (s + 1)] for s in range(4)]

        def turn_mu(pair):
            codes, scales = new_operand(("mu", pair), 2 * P)
            turn(("mu", pair), in_order[("mu", pair)], codes[:], scales[:])

        def turn_flow(i):
            codes, scales = new_operand(("flow", i), 2 * P)
            turn(("flow", i), in_order[("flow", i)], codes[:], scales[:])

        def turn_shift(h):
            j = h // 2
            if h % 2 == 0:
                new_operand(("shift", j), K_PASS)
            codes, scales = operands[("shift", j)]
            cols = slice(2 * P * (h % 2), 2 * P * (h % 2 + 1))
            bank = transposed(in_order[("shift", h)])
            grouped = stage.tile([P, SLAB], BF16, name="grouped_shift%d" % h, tag="grouped", align_bytes=ALIGN)
            nc.scalar.copy(
                out=grouped[:].bitcast(F32).rearrange("p (c v) -> p c v", v=4),
                in_=bank[:].rearrange("p (v c) -> p c v", c=P),
            )
            flush(lag=QUANT_LAG)
            quantise_later(("shift", j), codes[:, cols], scales[:, cols], grouped)

        lmp, open_banks = {}, {}

        def turn_lmp(i, chunks, copy_out=nc.scalar.copy):
            key = ("lmp", CHUNKS * i + chunks[0])
            codes, scales = new_operand(key, P * len(chunks))
            sources = []
            for a, j in enumerate(chunks):
                operands[("lmp", i, j)] = (key, codes[:, P * a : P * (a + 1)], scales[:, P * a : P * (a + 1)])
                words = lmp[(i, j)][:].bitcast(F32)
                sources.extend([words[:, P * u : P * (u + 1)] for u in range(2)])
            turn(key, sources, codes[:], scales[:], copy_out)

        delivery_row = kept("delivery_row", [P, N], BF16)
        strike_row = kept("strike_row", [P, Z], BF16)

        def spread_delivery():
            words = delivery_raw[:].bitcast(F32)
            rows = delivery_row[:].bitcast(F32).rearrange("m (j u q v) -> m u j q v", j=CHUNKS, u=2, v=4)
            for u in range(2):
                bank = next_bank()
                for v in range(4):
                    w = 2 * v + u
                    nc.tensor.transpose(bank[:, P * v : P * (v + 1)], words[:, w : w + 1].to_broadcast([P, P]), ident[:])
                nc.scalar.copy(out=rows[:, u], in_=bank[:].rearrange("m (v j q) -> m j q v", v=4, j=CHUNKS))

        def spread_strike():
            words = strike_raw[:].bitcast(F32)
            bank = next_bank()
            for w in range(2):
                nc.tensor.transpose(bank[:, P * w : P * (w + 1)], words[:, w : w + 1].to_broadcast([P, P]), ident[:])
            nc.scalar.activation(
                out=strike_row[:].rearrange("m (q w e) -> m q w e", w=2, e=2),
                in_=bank[:, : 2 * P].bitcast(BF16).rearrange("m (w q e) -> m q w e", w=2, e=2),
                func=ACT.Copy,
            )

        def congestion(i, j):
            flush([("mu", i // 2), ("shift", j)])
            bank = next_bank()
            cols = slice(P * (i % 2), P * (i % 2 + 1))
            mu_codes, mu_scales = operands[("mu", i // 2)]
            shift_codes, shift_scales = operands[("shift", j)]
            nc.tensor.matmul_mx(
                out=bank[:], lhsT=mu_codes[:, cols].bitcast(FP8X4), lhsT_scale=mu_scales[:, cols],
                rhs=shift_codes[:].bitcast(FP8X4), rhs_scale=shift_scales[:], start=True, stop=False,
            )
            open_banks[(i, j)] = bank

        def prices(i, j):
            if (i, j) not in open_banks:
                congestion(i, j)
            flush([("flow", i)])
            bank = open_banks[(i, j)]
            flow_codes, flow_scales = operands[("flow", i)]
            for g in range(2):
                cols = slice(P * g, P * (g + 1))
                nc.tensor.matmul_mx(
                    out=bank[:], lhsT=flow_codes[:, cols].bitcast(FP8X4), lhsT_scale=flow_scales[:, cols],
                    rhs=loss_codes[j][:, g, :].bitcast(FP4X4),
                    rhs_scale=loss_planes[j // 2][:, g, K_PASS * (j % 2) : K_PASS * (j % 2 + 1)], start=False, stop=(g == 1),
                )
            flush(lag=QUANT_LAG)
            lmp[(i, j)] = stage.tile([P, K_PASS], BF16, name="lmp_%d_%d" % (i, j), tag="lmp", bufs=16, align_bytes=ALIGN)
            sums = bank[:].rearrange("t (q u e) -> t u q e", u=2, e=2)
            sorted_lmp = lmp[(i, j)][:].rearrange("t (u q e) -> t u q e", u=2, e=2)
            sorted_delivery = delivery_row[:, K_PASS * j : K_PASS * (j + 1)].rearrange("t (u q e) -> t u q e", u=2, e=2)
            for u in range(2):
                nc.vector.scalar_tensor_tensor(
                    out=sorted_lmp[:, u], in0=sorted_delivery[:, u], scalar=energy_col[:, i : i + 1], in1=sums[:, u],
                    op0=ALU.mult, op1=ALU.add,
                )

        unclipped = []

        def clip_and_store():
            while unclipped:
                result, rows = unclipped.pop(0)
                nc.scalar.activation(out=result[:], in_=result[:], func=ACT.Relu)
                nc.sync.dma_start(out=rows, in_=result[:])

        def payoffs(i, groups=1, parts=1, lag=QUANT_LAG):
            width = Z // groups
            banks = [next_bank() for s in range(groups)]
            for half in range(2):
                for s in range(groups):
                    for j in (2 * half, 2 * half + 1):
                        key, codes, scales = operands[("lmp", i, j)]
                        flush([key])
                        nc.tensor.matmul_mx(
                            out=banks[s][:, :width], lhsT=codes.bitcast(FP8X4), lhsT_scale=scales,
                            rhs=pos_codes[:, j, 2 * width * s : 2 * width * (s + 1)].bitcast(FP4X4),
                            rhs_scale=pos_plane[:, j, width * s : width * (s + 1)],
                            start=(j == 0), stop=(j == CHUNKS - 1),
                        )
            flush(lag=lag)
            piece = Z // parts
            for s in range(parts):
                cols = slice(piece * s, piece * (s + 1))
                first = piece * s % width
                result = stage.tile([P, piece], F32, name="result_%d_%d" % (i, s), tag="result", bufs=8)
                nc.vector.tensor_tensor(
                    out=result[:], in0=banks[piece * s // width][:, first : first + piece], in1=strike_row[:, cols],
                    op=ALU.subtract,
                )
                clip_and_store()
                unclipped.append((result, out_rows[:, i, cols]))

        def run(turns, products, sorts=()):
            for work in turns:
                work[0](*work[1:])
            clip_and_store()
            for ahead in sorts:
                sort(*ahead)
            for work in products:
                work[0](*work[1:])

        V, S = nc.vector.tensor_copy, nc.scalar.copy
        spread_delivery()
        first = [(("mu", 0), turn_mu), (("shift", 0), turn_shift), (("shift", 1), turn_shift), (("flow", 0), turn_flow),
                 (("flow", 1), turn_flow), (("shift", 2), turn_shift), (("shift", 3), turn_shift)]
        sort(V, first[0][0])
        for n, (key, work) in enumerate(first[:-1]):
            sort(V, first[n + 1][0])
            work(key[1])
        run([], [(congestion, 0, 0), (congestion, 1, 0)])
        run([(turn_shift, 3)], [(prices, 0, 0), (flush, [("shift", 1)]), (prices, 1, 0)], [(V, ("mu", 1)), (V, ("flow", 2)), (S, ("flow", 3))])
        run([(turn_mu, 1), (turn_flow, 2)], [(prices, 0, 1), (prices, 1, 1)], [(S, ("shift", 4)), (S, ("shift", 5))])
        run([(turn_flow, 3), (turn_shift, 4), (turn_lmp, 0, (0, 1)), (turn_shift, 5), (turn_lmp, 1, (0, 1))],
            [(prices, 2, 0), (prices, 2, 1), (prices, 3, 0), (prices, 3, 1)],
            [(S, ("shift", 6)), (S, ("shift", 7)), (S, ("mu", 2)), (S, ("flow", 4))])
        run([(turn_shift, 6), (turn_shift, 7), (turn_mu, 2), (turn_flow, 4), (turn_lmp, 2, (0, 1)), (turn_lmp, 3, (0, 1))],
            [(prices, i, j) for j in (2, 3) for i in range(4)],
            [(S, ("flow", 5)), (S, ("mu", 3)), (S, ("flow", 6)), (S, ("flow", 7))])
        run([(turn_flow, 5), (turn_mu, 3), (turn_flow, 6), (turn_lmp, 0, (2, 3)), (turn_lmp, 1, (2, 3)), (turn_lmp, 2, (2, 3)), (spread_strike,)],
            [(prices, i, j) for i in (4, 5) for j in range(4)] + [(payoffs, 0), (payoffs, 1), (payoffs, 2)])
        run([(turn_flow, 7), (turn_lmp, 3, (2, 3))] + [(turn_lmp, i, half) for i in (4, 5) for half in ((0, 1), (2, 3))],
            [(prices, i, j) for i in (6, 7) for j in range(4)] + [(payoffs, 3), (payoffs, 4)])
        run([(turn_lmp, 6, (0, 1), V), (turn_lmp, 6, (2, 3)), (turn_lmp, 7, (0, 1)), (turn_lmp, 7, (2, 3))],
            [(payoffs, 5, 1, 1, 1), (payoffs, 6, 1, 2, 1), (payoffs, 7, 4, 4, 0)])
        clip_and_store()
